import numpy as np
import ml_dtypes


def mxq(x, axis, fmt="e4m3"):
    dtype, down = {"e4m3": (ml_dtypes.float8_e4m3fn, 7), "e5m2": (ml_dtypes.float8_e5m2, 14)}[fmt]
    v = np.moveaxis(np.asarray(x, np.float32).astype(ml_dtypes.bfloat16).astype(np.float64), axis, -1)
    blocks = v.reshape(v.shape[:-1] + (-1, 32))
    amax = np.abs(blocks).max(-1, keepdims=True)
    byte = np.maximum(np.where(amax > 0, np.frexp(amax)[1] - 1 + 127, 0) - down, 1)
    scale = np.exp2(byte - 127.0)
    codes = (blocks / scale).astype(np.float32).astype(dtype).astype(np.float64)
    return np.moveaxis((codes * scale).reshape(v.shape), -1, axis)


WIDE = False


def mx_kscale(k):
    if not WIDE:
        return np.ones(k)
    levels = np.array([10, -10, 5, -5, 0])
    if k % 512:
        return np.exp2(np.random.permutation(np.resize(levels, k // 32))).repeat(32)
    a = np.empty((k // 512, 16))
    for p in range(k // 512):
        a[p, :8] = np.random.permutation(np.resize(levels, 8))
        for g in range(8):
            far = levels[np.abs(levels - a[p, g]) >= 10]
            a[p, g + 8] = far[np.random.randint(len(far))]
    return np.exp2(a.ravel()).repeat(32)


def f64(x):
    return np.asarray(x).astype(np.float64)


def striped(idx):
    return np.tile(np.asarray(idx).reshape(-1, 16).T, (8, 1)).astype(np.uint16)


def unstriped(offs):
    return offs[:16].T.reshape(-1).astype(np.int64)


def striped8(idx):
    return np.asarray(idx).reshape(8, -1, 16).transpose(0, 2, 1).reshape(128, -1).astype(np.uint16)


def unstriped8(offs):
    return offs.reshape(8, 16, -1).transpose(0, 2, 1).reshape(8, -1).astype(np.int64)


def pick8(x, idx, run):
    r = np.arange(len(x))
    return x[r[:, None], idx[r % (8 * run) // run]]


E2M1 = np.array([0.0, 0.5, 1.0, 1.5, 2.0, 3.0, 4.0, 6.0, -0.0, -0.5, -1.0, -1.5, -2.0, -3.0, -4.0, -6.0])


def pack_weight(w, fmt):
    k, n = w.shape
    w = f64(np.asarray(w, np.float32).astype(ml_dtypes.bfloat16)).reshape(k // 32, 32, n)
    amax = np.abs(w).max(1)
    if fmt == "e4m3":
        byte = np.frexp(amax)[1] - 1 + 127 - 7
    else:
        mant, ex = np.frexp(amax / 6.0)
        byte = np.where(mant > 0.5, ex, ex - 1) + 127
    byte = np.clip(np.where(amax > 0, byte, 1), 1, 254)
    scaled = (w * np.exp2(127.0 - byte)[:, None, :]).reshape(k, n).astype(np.float32)
    by_word = np.ascontiguousarray(scaled.reshape(k // 512, 128, 4, n).transpose(0, 1, 3, 2))
    if fmt == "e4m3":
        words = by_word.astype(ml_dtypes.float8_e4m3fn).view(np.uint8)
    else:
        c = by_word.astype(ml_dtypes.float4_e2m1fn).view(np.uint8) & 0xF
        words = (c[..., 0::2] | (c[..., 1::2] << 4)).reshape(k // 512, 128, 2 * n)
    return np.ascontiguousarray(words), np.ascontiguousarray(byte.astype(np.uint8).reshape(k // 512, 16, n))


def unpack_weight(words, scales, fmt):
    g, _, n = scales.shape
    words = np.ascontiguousarray(words).reshape(g, 128, n, -1)
    if fmt == "e4m3":
        vals = words.view(ml_dtypes.float8_e4m3fn).astype(np.float64)
    else:
        nib = np.empty((g, 128, n, 4), np.uint8)
        nib[..., 0::2] = words & 0xF
        nib[..., 1::2] = words >> 4
        vals = E2M1[nib]
    vals = vals * np.repeat(np.exp2(scales.astype(np.float64) - 127.0), 8, axis=1)[..., None]
    return vals.transpose(0, 1, 3, 2).reshape(g * 512, n)


def sigmoid(v):
    return 1.0 / (1.0 + np.exp(-v))


K, R, F, T, J, M = 512, 128, 512, 2048, 512, 256


def setup_inputs():
    n = np.random.standard_normal
    idx = np.random.permutation(T)[:J]
    idx2 = np.stack([np.random.permutation(J)[:M] for _ in range(8)])
    idx3 = np.stack([np.random.permutation(J)[:M] for _ in range(8)])
    fk = mx_kscale(K)
    ff = mx_kscale(F)
    tabp = pack_weight(n((K, T)) / fk[:, None], "e4m3")
    return {
        "tab_words": tabp[0],
        "tab_scales": tabp[1],
        "w1": (n((K, R)) * 1 / np.sqrt(K) * fk[:, None]).astype(np.float32),
        "gain": (np.random.uniform(0.5, 1.5, (R, 1))).astype(np.float32),
        "wo": (n((F, R)) * 1 / np.sqrt(F) * ff[:, None]).astype(np.float32),
        "dy": (n((F, M)) / ff[:, None]).astype(np.float32),
        "old": (0.5 * n((R, J))).astype(np.float32),
        "offs": striped(idx),
        "offs2": striped8(idx2),
        "offs3": striped8(idx3),
    }


def reference(tab_words, tab_scales, w1, gain, wo, dy, old, offs, offs2, offs3):
    idx = unstriped(offs)
    idx2 = unstriped8(offs2)
    idx3 = unstriped8(offs3)
    tabu = unpack_weight(tab_words, tab_scales, "e4m3")
    w1q = mxq(f64(w1), 0, "e4m3")
    tabidxg = tabu[:, idx]
    a = w1q.T @ tabidxg
    h1 = a * f64(gain)
    woq = mxq(f64(wo), 0, "e4m3")
    dyq = mxq(f64(dy), 0, "e4m3")
    c0 = woq.T @ dyq
    e1 = c0 * sigmoid(pick8(h1, idx3, 16))
    s1 = np.zeros((R, J))
    s1[np.arange(R)[:, None], idx2[np.arange(R) % 128 // 16]] = e1
    e2 = c0 * pick8(h1, idx2, 16) * sigmoid(pick8(h1, idx3, 16)) * (1.0 - sigmoid(pick8(h1, idx3, 16)))
    s2 = np.zeros((R, J))
    s2[np.arange(R)[:, None], idx3[np.arange(R) % 128 // 16]] = e2
    e3 = c0 * (-1.0) * sigmoid(pick8(h1, idx3, 16))
    s3 = np.zeros((R, J))
    s3[np.arange(R)[:, None], idx3[np.arange(R) % 128 // 16]] = e3
    dh1 = s1 + s2 + s3
    da = dh1 * f64(gain)
    y = da + f64(old)
    return y

@@ -1,0 +1,111 @@
+from contextlib import ExitStack
+
+import concourse.mybir as mybir
+
+K, R, F, T, J, M = 512, 128, 512, 2048, 512, 256
+FLOPS = 2 * K * R * J + 2 * F * R * M
+
+F32 = mybir.dt.float32
+BF16 = mybir.dt.bfloat16
+I32 = mybir.dt.int32
+U32 = mybir.dt.uint32
+U16 = mybir.dt.uint16
+U8 = mybir.dt.uint8
+FP8X4 = mybir.dt.float8_e4m3fn_x4
+ALU = mybir.AluOpType
+ACT = mybir.ActivationFunctionType
+
+P = 128
+PACK = 4
+HALF = J // 2
+
+
+def tile_attend_cpairgates_kernel(tc, tab_words, tab_scales, w1, gain, wo, dy, old, offs, offs2, offs3, out):
+    nc = tc.nc
+    with ExitStack() as ctx:
+        lists = ctx.enter_context(tc.tile_pool(name="lists", bufs=1))
+        sb = ctx.enter_context(tc.tile_pool(name="sb", bufs=1))
+        ps = ctx.enter_context(tc.psum_pool(name="ps", bufs=1))
+
+        idx = lists.tile([P, J // 16], U16, name="idx")
+        idx2 = lists.tile([P, M // 16], U16, name="idx2")
+        idx3 = lists.tile([P, M // 16], U16, name="idx3")
+
+        tab_bytes = sb.tile([P, T], U8, name="tab_bytes", align_bytes=64)
+        tab_codes = sb.tile([P, T], I32, name="tab_codes", align_bytes=64)
+        w1_raw = sb.tile([P, PACK, R], F32, name="w1_raw")
+        wo_raw = sb.tile([P, PACK, R], F32, name="wo_raw")
+        dy_raw = sb.tile([P, PACK, M], F32, name="dy_raw")
+        gain_col = sb.tile([P, 1], F32, name="gain_col")
+        old_sb = sb.tile([P, J], F32, name="old_sb")
+        s1 = sb.tile([P, J], F32, name="s1")
+        s23 = sb.tile([P, J], F32, name="s23")
+
+        nc.vector.memset(tab_bytes[:].bitcast(I32), 0)
+        nc.sync.dma_start(idx[:], offs)
+        nc.sync.dma_start(w1_raw[:], w1.rearrange("(p t) r -> p t r", t=PACK))
+        for q in range(4):
+            nc.sync.dma_start(tab_bytes[32 * q : 32 * q + 4, :].bitcast(I32), tab_scales[0, 4 * q : 4 * q + 4, :].bitcast(I32))
+        nc.sync.dma_start(tab_codes[:], tab_words[0].rearrange("p n t -> p (n t)").bitcast(I32))
+        nc.sync.dma_start(dy_raw[:], dy.rearrange("(p t) m -> p t m", t=PACK))
+        nc.sync.dma_start(wo_raw[:], wo.rearrange("(p t) r -> p t r", t=PACK))
+        nc.sync.dma_start(gain_col[:], gain)
+        nc.sync.dma_start(idx3[:], offs3)
+        nc.sync.dma_start(idx2[:], offs2)
+        nc.sync.dma_start(old_sb[:], old)
+        nc.vector.memset(s1[:], 0.0)
+        nc.vector.memset(s23[:], 0.0)
+
+        def interleave(copy, raw, width, name):
+            grouped = sb.tile([P, width, PACK], BF16, name=name + "_bf", align_bytes=64)
+            copy(grouped[:], raw[:].rearrange("p t w -> p w t"))
+            return grouped
+
+        def quantise(grouped, width, name):
+            codes = sb.tile([P, width], U32, name=name + "_codes", align_bytes=64)
+            scales = sb.tile([P, width], U8, name=name + "_scales", align_bytes=64)
+            nc.vector.quantize_mx(codes[:].bitcast(FP8X4), scales[:], grouped[:].rearrange("p w t -> p (w t)"))
+            return codes, scales
+
+        w1_bf = interleave(nc.scalar.copy, w1_raw, R, "w1")
+        col_scales = sb.tile([P, J], U8, name="col_scales", align_bytes=64)
+        nc.vector.tensor_copy(col_scales[:], tab_bytes[:].indirect(idx[:]))
+        w1_codes, w1_scales = quantise(w1_bf, R, "w1")
+
+        col_codes = sb.tile([P, J], U32, name="col_codes", align_bytes=64)
+        h1 = sb.tile([P, J], F32, name="h1")
+        for u in range(2):
+            cols = slice(u * HALF, (u + 1) * HALF)
+            entries = slice(u * HALF // 16, (u + 1) * HALF // 16)
+            nc.vector.tensor_copy(col_codes[:, cols], tab_codes[:].bitcast(U32).indirect(idx[:, entries]))
+            a_ps = ps.tile([P, HALF], F32, name="a_ps%d" % u)
+            nc.tensor.matmul_mx(a_ps[:], lhsT=w1_codes[:].bitcast(FP8X4), lhsT_scale=w1_scales[:],
+                                rhs=col_codes[:, cols].bitcast(FP8X4), rhs_scale=col_scales[:, cols], start=True, stop=True)
+            nc.scalar.activation(h1[:, cols], a_ps[:], ACT.Copy, scale=gain_col[:])
+
+        sig = sb.tile([P, M], F32, name="sig")
+        nc.scalar.activation(sig[:], h1[:].indirect(idx3[:]), ACT.Sigmoid)
+
+        dy_bf = interleave(nc.vector.tensor_copy, dy_raw, M, "dy")
+        wo_bf = interleave(nc.vector.tensor_copy, wo_raw, R, "wo")
+        dy_codes, dy_scales = quantise(dy_bf, M, "dy")
+        wo_codes, wo_scales = quantise(wo_bf, R, "wo")
+        c0_ps = ps.tile([P, M], F32, name="c0_ps")
+        nc.tensor.matmul_mx(c0_ps[:], lhsT=wo_codes[:].bitcast(FP8X4), lhsT_scale=wo_scales[:],
+                            rhs=dy_codes[:].bitcast(FP8X4), rhs_scale=dy_scales[:], start=True, stop=True)
+
+        first = sb.tile([P, M], F32, name="first")
+        nc.vector.tensor_copy(first[:], h1[:].indirect(idx2[:]))
+        slope = sb.tile([P, M], F32, name="slope")
+        nc.vector.scalar_tensor_tensor(slope[:], sig[:], 1.0, first[:], ALU.subtract, ALU.mult)
+        e1 = sb.tile([P, M], F32, name="e1")
+        nc.vector.scalar_tensor_tensor(e1[:], c0_ps[:], gain_col[:], sig[:], ALU.mult, ALU.mult)
+        factor = sb.tile([P, M], F32, name="factor")
+        nc.scalar.activation(factor[:], slope[:], ACT.Copy, bias=-1.0, scale=-1.0)
+        nc.vector.tensor_copy(s1[:].indirect(idx2[:]), e1[:])
+        nc.vector.tensor_tensor(s23[:].indirect(idx3[:]), factor[:], e1[:], ALU.mult)
+        part = sb.tile([P, J], F32, name="part")
+        nc.vector.tensor_tensor(part[:], s1[:], old_sb[:], ALU.add)
+        y = sb.tile([P, J], F32, name="y")
+        nc.vector.tensor_tensor(y[:], part[:], s23[:], ALU.add)
+        nc.sync.dma_start(out, y[:])

@@ -1,6 +1,7 @@
 from contextlib import ExitStack
 
 import concourse.mybir as mybir
+from concourse.masks import make_identity
 
 K, R, F, T, J, M = 512, 128, 512, 2048, 512, 256
 FLOPS = 2 * K * R * J + 2 * F * R * M
@@ -35,42 +36,47 @@ def tile_attend_cpairgates_kernel(tc, tab_words, tab_scales, w1, gain, wo, dy, o
         tab_codes = sb.tile([P, T], I32, name="tab_codes", align_bytes=64)
         w1_raw = sb.tile([P, PACK, R], F32, name="w1_raw")
         wo_raw = sb.tile([P, PACK, R], F32, name="wo_raw")
-        dy_raw = sb.tile([P, PACK, M], F32, name="dy_raw")
+        dy_raw = sb.tile([P, PACK, M], F32, name="dy_raw", tag="staged")
         gain_col = sb.tile([P, 1], F32, name="gain_col")
-        old_sb = sb.tile([P, J], F32, name="old_sb")
         s1 = sb.tile([P, J], F32, name="s1")
         s23 = sb.tile([P, J], F32, name="s23")
 
         nc.vector.memset(tab_bytes[:].bitcast(I32), 0)
         nc.sync.dma_start(idx[:], offs)
         nc.sync.dma_start(w1_raw[:], w1.rearrange("(p t) r -> p t r", t=PACK))
+        nc.sync.dma_start(wo_raw[:], wo.rearrange("(p t) r -> p t r", t=PACK))
         for q in range(4):
             nc.sync.dma_start(tab_bytes[32 * q : 32 * q + 4, :].bitcast(I32), tab_scales[0, 4 * q : 4 * q + 4, :].bitcast(I32))
         nc.sync.dma_start(tab_codes[:], tab_words[0].rearrange("p n t -> p (n t)").bitcast(I32))
-        nc.sync.dma_start(dy_raw[:], dy.rearrange("(p t) m -> p t m", t=PACK))
-        nc.sync.dma_start(wo_raw[:], wo.rearrange("(p t) r -> p t r", t=PACK))
         nc.sync.dma_start(gain_col[:], gain)
+        nc.sync.dma_start(dy_raw[:], dy.rearrange("(p t) m -> p t m", t=PACK))
         nc.sync.dma_start(idx3[:], offs3)
         nc.sync.dma_start(idx2[:], offs2)
-        nc.sync.dma_start(old_sb[:], old)
         nc.vector.memset(s1[:], 0.0)
         nc.vector.memset(s23[:], 0.0)
+        warm = sb.tile([P, 1], F32, name="warm")
+        nc.scalar.activation(warm[:], s1[:, 0:1], ACT.Sigmoid)
+        ident = sb.tile([P, P], F32, name="ident")
+        nc.vector.memset(ident[:], 0.0)
+        make_identity(nc, ident[:], nomemset=True)
 
         def interleave(copy, raw, width, name):
-            grouped = sb.tile([P, width, PACK], BF16, name=name + "_bf", align_bytes=64)
-            copy(grouped[:], raw[:].rearrange("p t w -> p w t"))
+            grouped = sb.tile([P, width, PACK], BF16, name=name + "_bf", tag=name + "_bf", align_bytes=64)
+            copy(grouped[:].rearrange("p (c i) t -> p c t i", i=4), raw.rearrange("p t (c i) -> p c t i", i=4))
             return grouped
 
         def quantise(grouped, width, name):
-            codes = sb.tile([P, width], U32, name=name + "_codes", align_bytes=64)
+            codes = sb.tile([P, width], U32, name=name + "_codes", tag=name + "_codes", align_bytes=64)
             scales = sb.tile([P, width], U8, name=name + "_scales", align_bytes=64)
             nc.vector.quantize_mx(codes[:].bitcast(FP8X4), scales[:], grouped[:].rearrange("p w t -> p (w t)"))
             return codes, scales
 
-        w1_bf = interleave(nc.scalar.copy, w1_raw, R, "w1")
+        w1_bf = interleave(nc.scalar.copy, w1_raw[:], R, "w1")
+        wo_bf = interleave(nc.scalar.copy, wo_raw[:], R, "wo")
         col_scales = sb.tile([P, J], U8, name="col_scales", align_bytes=64)
         nc.vector.tensor_copy(col_scales[:], tab_bytes[:].indirect(idx[:]))
         w1_codes, w1_scales = quantise(w1_bf, R, "w1")
+        wo_codes, wo_scales = quantise(wo_bf, R, "wo")
 
         col_codes = sb.tile([P, J], U32, name="col_codes", align_bytes=64)
         h1 = sb.tile([P, J], F32, name="h1")
@@ -78,34 +84,50 @@ def tile_attend_cpairgates_kernel(tc, tab_words, tab_scales, w1, gain, wo, dy, o
             cols = slice(u * HALF, (u + 1) * HALF)
             entries = slice(u * HALF // 16, (u + 1) * HALF // 16)
             nc.vector.tensor_copy(col_codes[:, cols], tab_codes[:].bitcast(U32).indirect(idx[:, entries]))
-            a_ps = ps.tile([P, HALF], F32, name="a_ps%d" % u)
-            nc.tensor.matmul_mx(a_ps[:], lhsT=w1_codes[:].bitcast(FP8X4), lhsT_scale=w1_scales[:],
-                                rhs=col_codes[:, cols].bitcast(FP8X4), rhs_scale=col_scales[:, cols], start=True, stop=True)
-            nc.scalar.activation(h1[:, cols], a_ps[:], ACT.Copy, scale=gain_col[:])
+            width = HALF // (u + 1)
+            for c in range(u * HALF, (u + 1) * HALF, width):
+                part = slice(c, c + width)
+                a_ps = ps.tile([P, width], F32, name="a_ps%d" % c)
+                nc.tensor.matmul_mx(a_ps[:], lhsT=w1_codes[:].bitcast(FP8X4), lhsT_scale=w1_scales[:],
+                                    rhs=col_codes[:, part].bitcast(FP8X4), rhs_scale=col_scales[:, part], start=True, stop=True)
+                nc.scalar.activation(h1[:, part], a_ps[:], ACT.Copy, scale=gain_col[:])
 
         sig = sb.tile([P, M], F32, name="sig")
         nc.scalar.activation(sig[:], h1[:].indirect(idx3[:]), ACT.Sigmoid)
 
-        dy_bf = interleave(nc.vector.tensor_copy, dy_raw, M, "dy")
-        wo_bf = interleave(nc.vector.tensor_copy, wo_raw, R, "wo")
-        dy_codes, dy_scales = quantise(dy_bf, M, "dy")
-        wo_codes, wo_scales = quantise(wo_bf, R, "wo")
+        dy_bf = [interleave(nc.vector.tensor_copy, dy_raw[:, :, u * P : (u + 1) * P], P, "dy%d" % u) for u in range(2)]
+        old_sb = sb.tile([P, J], F32, name="old_sb", tag="staged")
+        nc.sync.dma_start(old_sb[:], old)
         c0_ps = ps.tile([P, M], F32, name="c0_ps")
-        nc.tensor.matmul_mx(c0_ps[:], lhsT=wo_codes[:].bitcast(FP8X4), lhsT_scale=wo_scales[:],
-                            rhs=dy_codes[:].bitcast(FP8X4), rhs_scale=dy_scales[:], start=True, stop=True)
+        for u in range(2):
+            dy_codes, dy_scales = quantise(dy_bf[u], P, "dy%d" % u)
+            nc.tensor.matmul_mx(c0_ps[:, u * P : (u + 1) * P], lhsT=wo_codes[:].bitcast(FP8X4), lhsT_scale=wo_scales[:],
+                                rhs=dy_codes[:].bitcast(FP8X4), rhs_scale=dy_scales[:], start=True, stop=True)
 
-        first = sb.tile([P, M], F32, name="first")
+        turned = [ps.tile([P, P], F32, name="turned%d" % b) for b in range(2)]
+        for b in range(2):
+            nc.tensor.matmul(turned[b][:], lhsT=old_sb[:, b * P : (b + 1) * P], rhs=ident[:], is_transpose=True, start=True, stop=False)
+        first = sb.tile([P, M], F32, name="first", tag="dy0_bf", align_bytes=64)
         nc.vector.tensor_copy(first[:], h1[:].indirect(idx2[:]))
-        slope = sb.tile([P, M], F32, name="slope")
-        nc.vector.scalar_tensor_tensor(slope[:], sig[:], 1.0, first[:], ALU.subtract, ALU.mult)
         e1 = sb.tile([P, M], F32, name="e1")
         nc.vector.scalar_tensor_tensor(e1[:], c0_ps[:], gain_col[:], sig[:], ALU.mult, ALU.mult)
+        slope = sb.tile([P, M], F32, name="slope", tag="dy1_codes", align_bytes=64)
+        nc.vector.scalar_tensor_tensor(slope[:], sig[:], 1.0, first[:], ALU.subtract, ALU.mult)
         factor = sb.tile([P, M], F32, name="factor")
         nc.scalar.activation(factor[:], slope[:], ACT.Copy, bias=-1.0, scale=-1.0)
         nc.vector.tensor_copy(s1[:].indirect(idx2[:]), e1[:])
         nc.vector.tensor_tensor(s23[:].indirect(idx3[:]), factor[:], e1[:], ALU.mult)
-        part = sb.tile([P, J], F32, name="part")
-        nc.vector.tensor_tensor(part[:], s1[:], old_sb[:], ALU.add)
+        part_t = sb.tile([P, HALF], F32, name="part_t", tag="late")
+        for b in range(2):
+            nc.tensor.matmul(turned[b][:], lhsT=s1[:, b * P : (b + 1) * P], rhs=ident[:], is_transpose=True, start=False, stop=True)
+            nc.scalar.copy(part_t[:, b * P : (b + 1) * P], turned[b][:])
+        left = ps.tile([P, HALF], F32, name="left")
+        for b in range(2):
+            nc.tensor.transpose(left[:, b * P : (b + 1) * P], part_t[:, b * P : (b + 1) * P], ident[:])
+        right = sb.tile([P, HALF], F32, name="right", tag="late")
+        nc.vector.tensor_tensor(right[:], s1[:, HALF:], old_sb[:, HALF:], ALU.add)
         y = sb.tile([P, J], F32, name="y")
-        nc.vector.tensor_tensor(y[:], part[:], s23[:], ALU.add)
-        nc.sync.dma_start(out, y[:])
+        for u, part in ((0, left), (1, right)):
+            cols = slice(u * HALF, (u + 1) * HALF)
+            nc.vector.tensor_tensor(y[:, cols], part[:], s23[:, cols], ALU.add)
+            nc.sync.dma_start(out[:, cols], y[:, cols])

@@ -37,25 +37,25 @@ def tile_attend_cpairgates_kernel(tc, tab_words, tab_scales, w1, gain, wo, dy, o
         w1_raw = sb.tile([P, PACK, R], F32, name="w1_raw")
         wo_raw = sb.tile([P, PACK, R], F32, name="wo_raw")
         dy_raw = sb.tile([P, PACK, M], F32, name="dy_raw", tag="staged")
-        gain_col = sb.tile([P, 1], F32, name="gain_col")
         s1 = sb.tile([P, J], F32, name="s1")
         s23 = sb.tile([P, J], F32, name="s23")
 
         nc.vector.memset(tab_bytes[:].bitcast(I32), 0)
-        nc.sync.dma_start(idx[:], offs)
         nc.sync.dma_start(w1_raw[:], w1.rearrange("(p t) r -> p t r", t=PACK))
+        nc.sync.dma_start(idx[:], offs)
         nc.sync.dma_start(wo_raw[:], wo.rearrange("(p t) r -> p t r", t=PACK))
         for q in range(4):
             nc.sync.dma_start(tab_bytes[32 * q : 32 * q + 4, :].bitcast(I32), tab_scales[0, 4 * q : 4 * q + 4, :].bitcast(I32))
         nc.sync.dma_start(tab_codes[:], tab_words[0].rearrange("p n t -> p (n t)").bitcast(I32))
-        nc.sync.dma_start(gain_col[:], gain)
         nc.sync.dma_start(dy_raw[:], dy.rearrange("(p t) m -> p t m", t=PACK))
         nc.sync.dma_start(idx3[:], offs3)
         nc.sync.dma_start(idx2[:], offs2)
         nc.vector.memset(s1[:], 0.0)
         nc.vector.memset(s23[:], 0.0)
-        warm = sb.tile([P, 1], F32, name="warm")
+        warm = sb.tile([P, 1], F32, name="warm", tag="column")
         nc.scalar.activation(warm[:], s1[:, 0:1], ACT.Sigmoid)
+        gain_col = sb.tile([P, 1], F32, name="gain_col", tag="column")
+        nc.gpsimd.dma_start(gain_col[:], gain)
         ident = sb.tile([P, P], F32, name="ident")
         nc.vector.memset(ident[:], 0.0)
         make_identity(nc, ident[:], nomemset=True)
@@ -117,17 +117,17 @@ def tile_attend_cpairgates_kernel(tc, tab_words, tab_scales, w1, gain, wo, dy, o
         nc.scalar.activation(factor[:], slope[:], ACT.Copy, bias=-1.0, scale=-1.0)
         nc.vector.tensor_copy(s1[:].indirect(idx2[:]), e1[:])
         nc.vector.tensor_tensor(s23[:].indirect(idx3[:]), factor[:], e1[:], ALU.mult)
-        part_t = sb.tile([P, HALF], F32, name="part_t", tag="late")
+        part_t = sb.tile([P, HALF], F32, name="part_t")
         for b in range(2):
             nc.tensor.matmul(turned[b][:], lhsT=s1[:, b * P : (b + 1) * P], rhs=ident[:], is_transpose=True, start=False, stop=True)
             nc.scalar.copy(part_t[:, b * P : (b + 1) * P], turned[b][:])
         left = ps.tile([P, HALF], F32, name="left")
         for b in range(2):
             nc.tensor.transpose(left[:, b * P : (b + 1) * P], part_t[:, b * P : (b + 1) * P], ident[:])
-        right = sb.tile([P, HALF], F32, name="right", tag="late")
+        right = sb.tile([P, HALF], F32, name="right", tag="dy1_codes", align_bytes=64)
         nc.vector.tensor_tensor(right[:], s1[:, HALF:], old_sb[:, HALF:], ALU.add)
         y = sb.tile([P, J], F32, name="y")
-        for u, part in ((0, left), (1, right)):
+        for u, part in ((1, right), (0, left)):
             cols = slice(u * HALF, (u + 1) * HALF)
             nc.vector.tensor_tensor(y[:, cols], part[:], s23[:, cols], ALU.add)
             nc.sync.dma_start(out[:, cols], y[:, cols])

@@ -36,18 +36,19 @@ def tile_attend_cpairgates_kernel(tc, tab_words, tab_scales, w1, gain, wo, dy, o
         tab_codes = sb.tile([P, T], I32, name="tab_codes", align_bytes=64)
         w1_raw = sb.tile([P, PACK, R], F32, name="w1_raw")
         wo_raw = sb.tile([P, PACK, R], F32, name="wo_raw")
-        dy_raw = sb.tile([P, PACK, M], F32, name="dy_raw", tag="staged")
+        dy_raw = [sb.tile([P, 2, M], F32, name="dy_raw%d" % v, tag="staged%d" % v) for v in range(2)]
         s1 = sb.tile([P, J], F32, name="s1")
         s23 = sb.tile([P, J], F32, name="s23")
 
         nc.vector.memset(tab_bytes[:].bitcast(I32), 0)
         nc.sync.dma_start(w1_raw[:], w1.rearrange("(p t) r -> p t r", t=PACK))
         nc.sync.dma_start(idx[:], offs)
-        nc.sync.dma_start(wo_raw[:], wo.rearrange("(p t) r -> p t r", t=PACK))
-        for q in range(4):
+        for q in (0, 2, 1, 3):
             nc.sync.dma_start(tab_bytes[32 * q : 32 * q + 4, :].bitcast(I32), tab_scales[0, 4 * q : 4 * q + 4, :].bitcast(I32))
         nc.sync.dma_start(tab_codes[:], tab_words[0].rearrange("p n t -> p (n t)").bitcast(I32))
-        nc.sync.dma_start(dy_raw[:], dy.rearrange("(p t) m -> p t m", t=PACK))
+        nc.sync.dma_start(wo_raw[:], wo.rearrange("(p t) r -> p t r", t=PACK))
+        for v in range(2):
+            nc.sync.dma_start(dy_raw[v][:], dy.rearrange("(p t) m -> p t m", t=PACK)[:, 2 * v : 2 * v + 2, :])
         nc.sync.dma_start(idx3[:], offs3)
         nc.sync.dma_start(idx2[:], offs2)
         nc.vector.memset(s1[:], 0.0)
@@ -72,11 +73,9 @@ def tile_attend_cpairgates_kernel(tc, tab_words, tab_scales, w1, gain, wo, dy, o
             return codes, scales
 
         w1_bf = interleave(nc.scalar.copy, w1_raw[:], R, "w1")
-        wo_bf = interleave(nc.scalar.copy, wo_raw[:], R, "wo")
         col_scales = sb.tile([P, J], U8, name="col_scales", align_bytes=64)
         nc.vector.tensor_copy(col_scales[:], tab_bytes[:].indirect(idx[:]))
         w1_codes, w1_scales = quantise(w1_bf, R, "w1")
-        wo_codes, wo_scales = quantise(wo_bf, R, "wo")
 
         col_codes = sb.tile([P, J], U32, name="col_codes", align_bytes=64)
         h1 = sb.tile([P, J], F32, name="h1")
@@ -95,8 +94,14 @@ def tile_attend_cpairgates_kernel(tc, tab_words, tab_scales, w1, gain, wo, dy, o
         sig = sb.tile([P, M], F32, name="sig")
         nc.scalar.activation(sig[:], h1[:].indirect(idx3[:]), ACT.Sigmoid)
 
-        dy_bf = [interleave(nc.vector.tensor_copy, dy_raw[:, :, u * P : (u + 1) * P], P, "dy%d" % u) for u in range(2)]
-        old_sb = sb.tile([P, J], F32, name="old_sb", tag="staged")
+        wo_bf = interleave(nc.scalar.copy, wo_raw[:], R, "wo")
+        wo_codes, wo_scales = quantise(wo_bf, R, "wo")
+        dy_bf = [sb.tile([P, P, PACK], BF16, name="dy%d_bf" % u, tag="dy%d_bf" % u, align_bytes=64) for u in range(2)]
+        for v in range(2):
+            for u in range(2):
+                nc.vector.tensor_copy(dy_bf[u][:, :, 2 * v : 2 * v + 2].rearrange("p (c i) t -> p c t i", i=4),
+                                      dy_raw[v][:, :, u * P : (u + 1) * P].rearrange("p t (c i) -> p c t i", i=4))
+        old_sb = sb.tile([P, J], F32, name="old_sb", tag="staged1")
         nc.sync.dma_start(old_sb[:], old)
         c0_ps = ps.tile([P, M], F32, name="c0_ps")
         for u in range(2):

from contextlib import ExitStack

import concourse.mybir as mybir
from concourse.masks import make_identity

K, R, F, T, J, M = 512, 128, 512, 2048, 512, 256
FLOPS = 2 * K * R * J + 2 * F * R * M

F32 = mybir.dt.float32
BF16 = mybir.dt.bfloat16
I32 = mybir.dt.int32
U32 = mybir.dt.uint32
U16 = mybir.dt.uint16
U8 = mybir.dt.uint8
FP8X4 = mybir.dt.float8_e4m3fn_x4
ALU = mybir.AluOpType
ACT = mybir.ActivationFunctionType

P = 128
PACK = 4
HALF = J // 2


def tile_attend_cpairgates_kernel(tc, tab_words, tab_scales, w1, gain, wo, dy, old, offs, offs2, offs3, out):
    nc = tc.nc
    with ExitStack() as ctx:
        lists = ctx.enter_context(tc.tile_pool(name="lists", bufs=1))
        sb = ctx.enter_context(tc.tile_pool(name="sb", bufs=1))
        ps = ctx.enter_context(tc.psum_pool(name="ps", bufs=1))

        idx = lists.tile([P, J // 16], U16, name="idx")
        idx2 = lists.tile([P, M // 16], U16, name="idx2")
        idx3 = lists.tile([P, M // 16], U16, name="idx3")

        tab_bytes = sb.tile([P, T], U8, name="tab_bytes", align_bytes=64)
        tab_codes = sb.tile([P, T], I32, name="tab_codes", align_bytes=64)
        w1_raw = sb.tile([P, PACK, R], F32, name="w1_raw")
        wo_raw = sb.tile([P, PACK, R], F32, name="wo_raw")
        dy_raw = [sb.tile([P, 2, M], F32, name="dy_raw%d" % v, tag="staged%d" % v) for v in range(2)]
        s1 = sb.tile([P, J], F32, name="s1")
        s23 = sb.tile([P, J], F32, name="s23")

        nc.vector.memset(tab_bytes[:].bitcast(I32), 0)
        nc.sync.dma_start(w1_raw[:], w1.rearrange("(p t) r -> p t r", t=PACK))
        nc.sync.dma_start(idx[:], offs)
        for q in (0, 2, 1, 3):
            nc.sync.dma_start(tab_bytes[32 * q : 32 * q + 4, :].bitcast(I32), tab_scales[0, 4 * q : 4 * q + 4, :].bitcast(I32))
        nc.sync.dma_start(tab_codes[:], tab_words[0].rearrange("p n t -> p (n t)").bitcast(I32))
        nc.sync.dma_start(wo_raw[:], wo.rearrange("(p t) r -> p t r", t=PACK))
        for v in range(2):
            nc.sync.dma_start(dy_raw[v][:], dy.rearrange("(p t) m -> p t m", t=PACK)[:, 2 * v : 2 * v + 2, :])
        nc.sync.dma_start(idx3[:], offs3)
        nc.sync.dma_start(idx2[:], offs2)
        nc.vector.memset(s1[:], 0.0)
        nc.vector.memset(s23[:], 0.0)
        warm = sb.tile([P, 1], F32, name="warm", tag="column")
        nc.scalar.activation(warm[:], s1[:, 0:1], ACT.Sigmoid)
        gain_col = sb.tile([P, 1], F32, name="gain_col", tag="column")
        nc.gpsimd.dma_start(gain_col[:], gain)
        ident = sb.tile([P, P], F32, name="ident")
        nc.vector.memset(ident[:], 0.0)
        make_identity(nc, ident[:], nomemset=True)

        def interleave(copy, raw, width, name):
            grouped = sb.tile([P, width, PACK], BF16, name=name + "_bf", tag=name + "_bf", align_bytes=64)
            copy(grouped[:].rearrange("p (c i) t -> p c t i", i=4), raw.rearrange("p t (c i) -> p c t i", i=4))
            return grouped

        def quantise(grouped, width, name):
            codes = sb.tile([P, width], U32, name=name + "_codes", tag=name + "_codes", align_bytes=64)
            scales = sb.tile([P, width], U8, name=name + "_scales", align_bytes=64)
            nc.vector.quantize_mx(codes[:].bitcast(FP8X4), scales[:], grouped[:].rearrange("p w t -> p (w t)"))
            return codes, scales

        w1_bf = interleave(nc.scalar.copy, w1_raw[:], R, "w1")
        col_scales = sb.tile([P, J], U8, name="col_scales", align_bytes=64)
        nc.vector.tensor_copy(col_scales[:], tab_bytes[:].indirect(idx[:]))
        w1_codes, w1_scales = quantise(w1_bf, R, "w1")

        col_codes = sb.tile([P, J], U32, name="col_codes", align_bytes=64)
        h1 = sb.tile([P, J], F32, name="h1")
        for u in range(2):
            cols = slice(u * HALF, (u + 1) * HALF)
            entries = slice(u * HALF // 16, (u + 1) * HALF // 16)
            nc.vector.tensor_copy(col_codes[:, cols], tab_codes[:].bitcast(U32).indirect(idx[:, entries]))
            width = HALF // (u + 1)
            for c in range(u * HALF, (u + 1) * HALF, width):
                part = slice(c, c + width)
                a_ps = ps.tile([P, width], F32, name="a_ps%d" % c)
                nc.tensor.matmul_mx(a_ps[:], lhsT=w1_codes[:].bitcast(FP8X4), lhsT_scale=w1_scales[:],
                                    rhs=col_codes[:, part].bitcast(FP8X4), rhs_scale=col_scales[:, part], start=True, stop=True)
                nc.scalar.activation(h1[:, part], a_ps[:], ACT.Copy, scale=gain_col[:])

        sig = sb.tile([P, M], F32, name="sig")
        nc.scalar.activation(sig[:], h1[:].indirect(idx3[:]), ACT.Sigmoid)

        wo_bf = interleave(nc.scalar.copy, wo_raw[:], R, "wo")
        wo_codes, wo_scales = quantise(wo_bf, R, "wo")
        dy_bf = [sb.tile([P, P, PACK], BF16, name="dy%d_bf" % u, tag="dy%d_bf" % u, align_bytes=64) for u in range(2)]
        for v in range(2):
            for u in range(2):
                nc.vector.tensor_copy(dy_bf[u][:, :, 2 * v : 2 * v + 2].rearrange("p (c i) t -> p c t i", i=4),
                                      dy_raw[v][:, :, u * P : (u + 1) * P].rearrange("p t (c i) -> p c t i", i=4))
        old_sb = sb.tile([P, J], F32, name="old_sb", tag="staged1")
        nc.sync.dma_start(old_sb[:], old)
        c0_ps = ps.tile([P, M], F32, name="c0_ps")
        for u in range(2):
            dy_codes, dy_scales = quantise(dy_bf[u], P, "dy%d" % u)
            nc.tensor.matmul_mx(c0_ps[:, u * P : (u + 1) * P], lhsT=wo_codes[:].bitcast(FP8X4), lhsT_scale=wo_scales[:],
                                rhs=dy_codes[:].bitcast(FP8X4), rhs_scale=dy_scales[:], start=True, stop=True)

        turned = [ps.tile([P, P], F32, name="turned%d" % b) for b in range(2)]
        for b in range(2):
            nc.tensor.matmul(turned[b][:], lhsT=old_sb[:, b * P : (b + 1) * P], rhs=ident[:], is_transpose=True, start=True, stop=False)
        first = sb.tile([P, M], F32, name="first", tag="dy0_bf", align_bytes=64)
        nc.vector.tensor_copy(first[:], h1[:].indirect(idx2[:]))
        e1 = sb.tile([P, M], F32, name="e1")
        nc.vector.scalar_tensor_tensor(e1[:], c0_ps[:], gain_col[:], sig[:], ALU.mult, ALU.mult)
        slope = sb.tile([P, M], F32, name="slope", tag="dy1_codes", align_bytes=64)
        nc.vector.scalar_tensor_tensor(slope[:], sig[:], 1.0, first[:], ALU.subtract, ALU.mult)
        factor = sb.tile([P, M], F32, name="factor")
        nc.scalar.activation(factor[:], slope[:], ACT.Copy, bias=-1.0, scale=-1.0)
        nc.vector.tensor_copy(s1[:].indirect(idx2[:]), e1[:])
        nc.vector.tensor_tensor(s23[:].indirect(idx3[:]), factor[:], e1[:], ALU.mult)
        part_t = sb.tile([P, HALF], F32, name="part_t")
        for b in range(2):
            nc.tensor.matmul(turned[b][:], lhsT=s1[:, b * P : (b + 1) * P], rhs=ident[:], is_transpose=True, start=False, stop=True)
            nc.scalar.copy(part_t[:, b * P : (b + 1) * P], turned[b][:])
        left = ps.tile([P, HALF], F32, name="left")
        for b in range(2):
            nc.tensor.transpose(left[:, b * P : (b + 1) * P], part_t[:, b * P : (b + 1) * P], ident[:])
        right = sb.tile([P, HALF], F32, name="right", tag="dy1_codes", align_bytes=64)
        nc.vector.tensor_tensor(right[:], s1[:, HALF:], old_sb[:, HALF:], ALU.add)
        y = sb.tile([P, J], F32, name="y")
        for u, part in ((1, right), (0, left)):
            cols = slice(u * HALF, (u + 1) * HALF)
            nc.vector.tensor_tensor(y[:, cols], part[:], s23[:, cols], ALU.add)
            nc.sync.dma_start(out[:, cols], y[:, cols])
